import numpy as np, ml_dtypes
CORES = [8,136,40,168]
N = 4
TK, LAY = 64, 2
def setup_inputs(rng):
    return {"x": rng.standard_normal((N, 128, TK), dtype=np.float32).astype(ml_dtypes.bfloat16), "wu": (rng.standard_normal((N, 128, LAY * 256), dtype=np.float32) / 16).astype(ml_dtypes.bfloat16), "wd": (rng.standard_normal((N, 128, 256), dtype=np.float32) / 16).astype(ml_dtypes.bfloat16)}
def setup_inputs_big(rng):
    d = setup_inputs(rng)
    for k in ("x",): d[k] = (d[k].astype(np.float32) * 1048576.0).astype(d[k].dtype)
    return d
def setup_inputs_small(rng):
    d = setup_inputs(rng)
    for k in ("x",): d[k] = (d[k].astype(np.float32) * (1 / 1048576.0)).astype(d[k].dtype)
    return d
def setup_inputs_apart(rng):
    d = setup_inputs(rng)
    f = (10.0 ** rng.permutation(np.linspace(-1.5, 1.5, N))).astype(np.float32).reshape(N, 1, 1)
    for k in ("x",): d[k] = (d[k].astype(np.float32) * f).astype(d[k].dtype)
    return d
def reference(x, wu, wd):
    X, WU, WD = x.astype(np.float64), wu.astype(np.float64), wd.astype(np.float64)
    s = list(X)
    for l in range(LAY):
        for q in range(0, N, 2 << l):
            p = q + (1 << l)
            s[q] = np.maximum(WU[q][:, 256 * l:256 * l + 128].T @ s[q] + WU[q][:, 256 * l + 128:256 * l + 256].T @ s[p], 0.0)
    for l in range(LAY - 1, -1, -1):
        for q in range(0, N, 2 << l):
            p = q + (1 << l)
            s[p] = np.maximum(WD[p][:, 0:128].T @ s[p] + WD[p][:, 128:256].T @ s[q], 0.0)
    return {"y": np.stack(s).astype(ml_dtypes.bfloat16)}

@@ -1,0 +1,145 @@
+from concourse.bass import DstId, RemoteDMATransfer
+from concourse.mybir import AluOpType
+
+TK = 64
+W = 128
+PK = TK + 4 * W
+
+SCRATCH = {
+    "pk":   ("sbuf", [128, PK], "bfloat16"),
+    "rpk":  ("sbuf", [128, PK], "bfloat16"),
+    "rx1":  ("sbuf", [128, TK], "bfloat16"),
+    "rx3":  ("sbuf", [128, TK], "bfloat16"),
+    "wdn":  ("sbuf", [128, 2 * W], "bfloat16"),
+    "fin":  ("sbuf", [128, TK], "bfloat16"),
+    "s0":   ("sbuf", [128, TK], "bfloat16"),
+    "s2":   ("sbuf", [128, TK], "bfloat16"),
+    "t0":   ("sbuf", [128, TK], "bfloat16"),
+    "t2":   ("sbuf", [128, TK], "bfloat16"),
+    "zero": ("sbuf", [128, TK], "float32"),
+    "pa":   ("psum", [128, 512], "float32"),
+    "pb":   ("psum", [128, 512], "float32"),
+    "pc":   ("psum", [128, 512], "float32"),
+    "pd":   ("psum", [128, 512], "float32"),
+}
+SEMAPHORES = ["ld", "ldd", "zs", "a1", "a3", "aw", "af", "sent", "st",
+              "ma", "mb", "mc", "md", "va", "vb", "vc", "vd"]
+
+
+def rank_program(g, core, T, topo):
+    rank = T.rank_of(core)
+    if rank is None:
+        return
+    S = T.sem
+    te, ve, sy, sc = g.tensor, g.vector, g.sync, g.scalar
+
+    def tile(buf, k):
+        return buf[:, TK + k * W: TK + (k + 1) * W]
+
+    def lanes(dst):
+        m = topo.mask(core, dst)
+        return m, bin(m).count("1")
+
+    def send(r, out, src, sem):
+        dst = T.cores[r]
+        rid, pid = topo.addr(dst, core)
+        m, n = lanes(dst)
+        g.remote_dma(out_ap=out, in_ap=src, remote_sem=sem, local_sem=S.sent, pid=pid, routing_id=rid,
+                     dma_engine_mask=m)
+        return n
+
+    def arrived(sem, r):
+        te.wait_ge(sem, lanes_from(r))
+
+    def lanes_from(r):
+        return bin(topo.mask(T.cores[r], core)).count("1")
+
+    def relu(out, acc, after, done):
+        ve.wait_ge(after, 1)
+        ve.tensor_tensor(out[:], acc[:, 0:TK], T.zero[:], AluOpType.max).then_inc(done, 1)
+
+    ve.memset(T.zero[:], 0.0).then_inc(S.zs, 1)
+    ve.wait_ge(S.zs, 1)
+
+    if rank % 2 == 1:
+        sy.dma_start(T.pk[:, 0:TK], T.x[:]).then_inc(S.ld, 16)
+        sy.dma_start(T.wdn[:], T.wd[:]).then_inc(S.ldd, 16)
+        land, sem = (T.rx1, S.a1) if rank == 1 else (T.rx3, S.a3)
+        ids = []
+        for r in (0, 2):
+            rid, pid = topo.addr(T.cores[r], core)
+            ids.append(DstId(rid=rid, pnc=pid))
+        m, n = lanes(T.cores[0])
+        g.wait_ge(S.ld, 16)
+        g.remote_dma_fused([RemoteDMATransfer(dst_ids=ids, dma_engine_mask=m, remote_sem=sem,
+                                              srcs=[T.pk[:, 0:TK]], dsts=[land[:], land[:]])], local_sem=S.sent)
+        te.wait_ge(S.ld, 16)
+        te.wait_ge(S.ldd, 16)
+        te.matmul(T.pa[:, 0:TK], T.wdn[:, 0:W], T.pk[:, 0:TK], True, False)
+        arrived(S.af, rank - 1)
+        te.matmul(T.pa[:, 0:TK], T.wdn[:, W:2 * W], T.fin[:], False, True).then_inc(S.ma, 1)
+        relu(T.t0, T.pa, S.ma, S.va)
+        sy.wait_ge(S.va, 1)
+        sy.dma_start(T.y[:], T.t0[:]).then_inc(S.st, 16)
+        sy.wait_ge(S.st, 16)
+        g.wait_ge(S.sent, n)
+        return
+
+    if rank == 0:
+        sy.dma_start(T.pk[:, 0:TK], T.x[:]).then_inc(S.ld, 16)
+        sc.dma_start(T.pk[:, TK:PK], T.wu[:]).then_inc(S.ld, 16)
+        g.wait_ge(S.ld, 32)
+        left = send(2, T.rpk[:], T.pk[:], S.aw)
+        te.wait_ge(S.ld, 32)
+        te.matmul(T.pa[:, 0:TK], tile(T.pk, 0), T.pk[:, 0:TK], True, False)
+        arrived(S.a1, 1)
+        te.matmul(T.pa[:, 0:TK], tile(T.pk, 1), T.rx1[:], False, True).then_inc(S.ma, 1)
+        relu(T.s0, T.pa, S.ma, S.va)
+        te.wait_ge(S.va, 1)
+        te.matmul(T.pc[:, 0:TK], tile(T.pk, 2), T.s0[:], True, False)
+        arrived(S.a3, 3)
+        arrived(S.aw, 2)
+        te.matmul(T.pb[:, 0:TK], tile(T.rpk, 0), T.rpk[:, 0:TK], True, False)
+        te.matmul(T.pb[:, 0:TK], tile(T.rpk, 1), T.rx3[:], False, True).then_inc(S.mb, 1)
+        relu(T.s2, T.pb, S.mb, S.vb)
+        te.wait_ge(S.vb, 1)
+        te.matmul(T.pc[:, 0:TK], tile(T.pk, 3), T.s2[:], False, True).then_inc(S.mc, 1)
+        relu(T.t0, T.pc, S.mc, S.vc)
+        g.wait_ge(S.vc, 1)
+        left += send(1, T.fin[:], T.t0[:], S.af)
+        out = T.t0
+    else:
+        half = TK + 2 * W
+        sy.dma_start(T.pk[:, 0:TK], T.x[:]).then_inc(S.ld, 16)
+        sc.dma_start(T.pk[:, TK:half], T.wu[:, 0:2 * W]).then_inc(S.ld, 16)
+        sc.dma_start(T.wdn[:], T.wd[:]).then_inc(S.ldd, 16)
+        g.wait_ge(S.ld, 32)
+        left = send(0, T.rpk[:, 0:half], T.pk[:, 0:half], S.aw)
+        te.wait_ge(S.ld, 32)
+        te.matmul(T.pb[:, 0:TK], tile(T.pk, 0), T.pk[:, 0:TK], True, False)
+        arrived(S.a3, 3)
+        te.matmul(T.pb[:, 0:TK], tile(T.pk, 1), T.rx3[:], False, True).then_inc(S.mb, 1)
+        relu(T.s2, T.pb, S.mb, S.vb)
+        te.wait_ge(S.vb, 1)
+        te.wait_ge(S.ldd, 16)
+        te.matmul(T.pd[:, 0:TK], T.wdn[:, 0:W], T.s2[:], True, False)
+        arrived(S.a1, 1)
+        arrived(S.aw, 0)
+        te.matmul(T.pa[:, 0:TK], tile(T.rpk, 0), T.rpk[:, 0:TK], True, False)
+        te.matmul(T.pa[:, 0:TK], tile(T.rpk, 1), T.rx1[:], False, True).then_inc(S.ma, 1)
+        te.matmul(T.pc[:, 0:TK], tile(T.rpk, 3), T.s2[:], True, False)
+        relu(T.s0, T.pa, S.ma, S.va)
+        te.wait_ge(S.va, 1)
+        te.matmul(T.pc[:, 0:TK], tile(T.rpk, 2), T.s0[:], False, True).then_inc(S.mc, 1)
+        relu(T.t0, T.pc, S.mc, S.vc)
+        te.wait_ge(S.vc, 1)
+        te.matmul(T.pd[:, 0:TK], T.wdn[:, W:2 * W], T.t0[:], False, True).then_inc(S.md, 1)
+        relu(T.t2, T.pd, S.md, S.vd)
+        g.wait_ge(S.vd, 1)
+        left += send(3, T.fin[:], T.t2[:], S.af)
+        out = T.t2
+
+    sy.wait_ge(S.sent, left)
+    sy.dma_start(T.y[:], out[:]).then_inc(S.st, 16)
+    sy.wait_ge(S.st, 16)
+    g.wait_ge(S.sent, left)

@@ -1,29 +1,36 @@
-from concourse.bass import DstId, RemoteDMATransfer
 from concourse.mybir import AluOpType
 
 TK = 64
 W = 128
+HALF = TK + 2 * W
 PK = TK + 4 * W
 
 SCRATCH = {
     "pk":   ("sbuf", [128, PK], "bfloat16"),
-    "rpk":  ("sbuf", [128, PK], "bfloat16"),
+    "wdn":  ("sbuf", [128, 2 * W], "bfloat16"),
+    "rp2":  ("sbuf", [128, HALF], "bfloat16"),
+    "ruv":  ("sbuf", [128, 2 * W], "bfloat16"),
+    "rde":  ("sbuf", [128, 2 * W], "bfloat16"),
     "rx1":  ("sbuf", [128, TK], "bfloat16"),
     "rx3":  ("sbuf", [128, TK], "bfloat16"),
-    "wdn":  ("sbuf", [128, 2 * W], "bfloat16"),
-    "fin":  ("sbuf", [128, TK], "bfloat16"),
+    "rs0":  ("sbuf", [128, TK], "bfloat16"),
+    "rs2":  ("sbuf", [128, TK], "bfloat16"),
+    "rt0":  ("sbuf", [128, TK], "bfloat16"),
     "s0":   ("sbuf", [128, TK], "bfloat16"),
     "s2":   ("sbuf", [128, TK], "bfloat16"),
     "t0":   ("sbuf", [128, TK], "bfloat16"),
     "t2":   ("sbuf", [128, TK], "bfloat16"),
+    "yo":   ("sbuf", [128, TK], "bfloat16"),
     "zero": ("sbuf", [128, TK], "float32"),
     "pa":   ("psum", [128, 512], "float32"),
     "pb":   ("psum", [128, 512], "float32"),
     "pc":   ("psum", [128, 512], "float32"),
     "pd":   ("psum", [128, 512], "float32"),
+    "pe":   ("psum", [128, 512], "float32"),
 }
-SEMAPHORES = ["ld", "ldd", "zs", "a1", "a3", "aw", "af", "sent", "st",
-              "ma", "mb", "mc", "md", "va", "vb", "vc", "vd"]
+SEMAPHORES = ["ld", "lduv", "ldd", "zs", "sent", "st",
+              "ax1", "ax3", "ap2", "auv", "ade", "as0", "as2", "at0",
+              "ma", "mb", "mc", "md", "me", "va", "vb", "vc", "vd", "ve"]
 
 
 def rank_program(g, core, T, topo):
@@ -32,114 +39,131 @@ def rank_program(g, core, T, topo):
         return
     S = T.sem
     te, ve, sy, sc = g.tensor, g.vector, g.sync, g.scalar
+    X = T.pk[:, 0:TK]
+    left = [0]
 
     def tile(buf, k):
         return buf[:, TK + k * W: TK + (k + 1) * W]
 
-    def lanes(dst):
-        m = topo.mask(core, dst)
-        return m, bin(m).count("1")
-
     def send(r, out, src, sem):
         dst = T.cores[r]
         rid, pid = topo.addr(dst, core)
-        m, n = lanes(dst)
+        m = topo.mask(core, dst)
         g.remote_dma(out_ap=out, in_ap=src, remote_sem=sem, local_sem=S.sent, pid=pid, routing_id=rid,
                      dma_engine_mask=m)
-        return n
+        left[0] += bin(m).count("1")
 
     def arrived(sem, r):
-        te.wait_ge(sem, lanes_from(r))
+        te.wait_ge(sem, bin(topo.mask(T.cores[r], core)).count("1"))
 
-    def lanes_from(r):
-        return bin(topo.mask(T.cores[r], core)).count("1")
+    def mm(acc, w, s, first, last):
+        return te.matmul(acc[:, 0:TK], w, s, first, last)
 
     def relu(out, acc, after, done):
         ve.wait_ge(after, 1)
         ve.tensor_tensor(out[:], acc[:, 0:TK], T.zero[:], AluOpType.max).then_inc(done, 1)
 
+    def store(out, ready, n):
+        sy.wait_ge(ready, n)
+        sy.dma_start(T.y[:], out[:]).then_inc(S.st, 16)
+        sy.wait_ge(S.st, 16)
+        g.wait_ge(S.sent, left[0])
+
     ve.memset(T.zero[:], 0.0).then_inc(S.zs, 1)
     ve.wait_ge(S.zs, 1)
 
-    if rank % 2 == 1:
-        sy.dma_start(T.pk[:, 0:TK], T.x[:]).then_inc(S.ld, 16)
-        sy.dma_start(T.wdn[:], T.wd[:]).then_inc(S.ldd, 16)
-        land, sem = (T.rx1, S.a1) if rank == 1 else (T.rx3, S.a3)
-        ids = []
-        for r in (0, 2):
-            rid, pid = topo.addr(T.cores[r], core)
-            ids.append(DstId(rid=rid, pnc=pid))
-        m, n = lanes(T.cores[0])
-        g.wait_ge(S.ld, 16)
-        g.remote_dma_fused([RemoteDMATransfer(dst_ids=ids, dma_engine_mask=m, remote_sem=sem,
-                                              srcs=[T.pk[:, 0:TK]], dsts=[land[:], land[:]])], local_sem=S.sent)
-        te.wait_ge(S.ld, 16)
-        te.wait_ge(S.ldd, 16)
-        te.matmul(T.pa[:, 0:TK], T.wdn[:, 0:W], T.pk[:, 0:TK], True, False)
-        arrived(S.af, rank - 1)
-        te.matmul(T.pa[:, 0:TK], T.wdn[:, W:2 * W], T.fin[:], False, True).then_inc(S.ma, 1)
-        relu(T.t0, T.pa, S.ma, S.va)
-        sy.wait_ge(S.va, 1)
-        sy.dma_start(T.y[:], T.t0[:]).then_inc(S.st, 16)
-        sy.wait_ge(S.st, 16)
-        g.wait_ge(S.sent, n)
-        return
-
     if rank == 0:
-        sy.dma_start(T.pk[:, 0:TK], T.x[:]).then_inc(S.ld, 16)
-        sc.dma_start(T.pk[:, TK:PK], T.wu[:]).then_inc(S.ld, 16)
-        g.wait_ge(S.ld, 32)
-        left = send(2, T.rpk[:], T.pk[:], S.aw)
+        sc.dma_start(T.pk[:, HALF:PK], T.wu[:, 2 * W:4 * W]).then_inc(S.lduv, 16)
+        sy.dma_start(X, T.x[:]).then_inc(S.ld, 16)
+        sy.dma_start(T.pk[:, TK:HALF], T.wu[:, 0:2 * W]).then_inc(S.ld, 16)
+        g.wait_ge(S.lduv, 16)
+        send(3, T.ruv[:], T.pk[:, HALF:PK], S.auv)
+        send(2, T.ruv[:], T.pk[:, HALF:PK], S.auv)
         te.wait_ge(S.ld, 32)
-        te.matmul(T.pa[:, 0:TK], tile(T.pk, 0), T.pk[:, 0:TK], True, False)
-        arrived(S.a1, 1)
-        te.matmul(T.pa[:, 0:TK], tile(T.pk, 1), T.rx1[:], False, True).then_inc(S.ma, 1)
+        mm(T.pa, tile(T.pk, 0), X, True, False)
+        arrived(S.ax1, 1)
+        mm(T.pa, tile(T.pk, 1), T.rx1[:], False, True).then_inc(S.ma, 1)
         relu(T.s0, T.pa, S.ma, S.va)
+        g.wait_ge(S.va, 1)
+        send(3, T.rs0[:], T.s0[:], S.as0)
+        send(2, T.rs0[:], T.s0[:], S.as0)
         te.wait_ge(S.va, 1)
-        te.matmul(T.pc[:, 0:TK], tile(T.pk, 2), T.s0[:], True, False)
-        arrived(S.a3, 3)
-        arrived(S.aw, 2)
-        te.matmul(T.pb[:, 0:TK], tile(T.rpk, 0), T.rpk[:, 0:TK], True, False)
-        te.matmul(T.pb[:, 0:TK], tile(T.rpk, 1), T.rx3[:], False, True).then_inc(S.mb, 1)
+        te.wait_ge(S.lduv, 16)
+        mm(T.pc, tile(T.pk, 2), T.s0[:], True, False)
+        arrived(S.ax3, 3)
+        arrived(S.ap2, 2)
+        mm(T.pb, tile(T.rp2, 0), T.rp2[:, 0:TK], True, False)
+        mm(T.pb, tile(T.rp2, 1), T.rx3[:], False, True).then_inc(S.mb, 1)
         relu(T.s2, T.pb, S.mb, S.vb)
         te.wait_ge(S.vb, 1)
-        te.matmul(T.pc[:, 0:TK], tile(T.pk, 3), T.s2[:], False, True).then_inc(S.mc, 1)
+        mm(T.pc, tile(T.pk, 3), T.s2[:], False, True).then_inc(S.mc, 1)
         relu(T.t0, T.pc, S.mc, S.vc)
         g.wait_ge(S.vc, 1)
-        left += send(1, T.fin[:], T.t0[:], S.af)
-        out = T.t0
-    else:
-        half = TK + 2 * W
-        sy.dma_start(T.pk[:, 0:TK], T.x[:]).then_inc(S.ld, 16)
-        sc.dma_start(T.pk[:, TK:half], T.wu[:, 0:2 * W]).then_inc(S.ld, 16)
-        sc.dma_start(T.wdn[:], T.wd[:]).then_inc(S.ldd, 16)
+        send(1, T.rt0[:], T.t0[:], S.at0)
+        store(T.t0, S.sent, left[0])
+
+    elif rank == 2:
+        sy.dma_start(X, T.x[:]).then_inc(S.ld, 16)
+        sc.dma_start(T.pk[:, TK:HALF], T.wu[:, 0:2 * W]).then_inc(S.ld, 16)
+        sy.dma_start(T.wdn[:], T.wd[:]).then_inc(S.ldd, 16)
         g.wait_ge(S.ld, 32)
-        left = send(0, T.rpk[:, 0:half], T.pk[:, 0:half], S.aw)
+        send(0, T.rp2[:], T.pk[:, 0:HALF], S.ap2)
+        g.wait_ge(S.ldd, 16)
+        send(3, T.rde[:], T.wdn[:], S.ade)
         te.wait_ge(S.ld, 32)
-        te.matmul(T.pb[:, 0:TK], tile(T.pk, 0), T.pk[:, 0:TK], True, False)
-        arrived(S.a3, 3)
-        te.matmul(T.pb[:, 0:TK], tile(T.pk, 1), T.rx3[:], False, True).then_inc(S.mb, 1)
+        mm(T.pb, tile(T.pk, 0), X, True, False)
+        arrived(S.ax3, 3)
+        mm(T.pb, tile(T.pk, 1), T.rx3[:], False, True).then_inc(S.mb, 1)
         relu(T.s2, T.pb, S.mb, S.vb)
+        g.wait_ge(S.vb, 1)
+        send(3, T.rs2[:], T.s2[:], S.as2)
         te.wait_ge(S.vb, 1)
         te.wait_ge(S.ldd, 16)
-        te.matmul(T.pd[:, 0:TK], T.wdn[:, 0:W], T.s2[:], True, False)
-        arrived(S.a1, 1)
-        arrived(S.aw, 0)
-        te.matmul(T.pa[:, 0:TK], tile(T.rpk, 0), T.rpk[:, 0:TK], True, False)
-        te.matmul(T.pa[:, 0:TK], tile(T.rpk, 1), T.rx1[:], False, True).then_inc(S.ma, 1)
-        te.matmul(T.pc[:, 0:TK], tile(T.rpk, 3), T.s2[:], True, False)
-        relu(T.s0, T.pa, S.ma, S.va)
-        te.wait_ge(S.va, 1)
-        te.matmul(T.pc[:, 0:TK], tile(T.rpk, 2), T.s0[:], False, True).then_inc(S.mc, 1)
+        mm(T.pd, T.wdn[:, 0:W], T.s2[:], True, False)
+        arrived(S.auv, 0)
+        mm(T.pc, T.ruv[:, W:2 * W], T.s2[:], True, False)
+        arrived(S.as0, 0)
+        mm(T.pc, T.ruv[:, 0:W], T.rs0[:], False, True).then_inc(S.mc, 1)
         relu(T.t0, T.pc, S.mc, S.vc)
         te.wait_ge(S.vc, 1)
-        te.matmul(T.pd[:, 0:TK], T.wdn[:, W:2 * W], T.t0[:], False, True).then_inc(S.md, 1)
+        mm(T.pd, T.wdn[:, W:2 * W], T.t0[:], False, True).then_inc(S.md, 1)
         relu(T.t2, T.pd, S.md, S.vd)
-        g.wait_ge(S.vd, 1)
-        left += send(3, T.fin[:], T.t2[:], S.af)
-        out = T.t2
+        store(T.t2, S.vd, 1)
 
-    sy.wait_ge(S.sent, left)
-    sy.dma_start(T.y[:], out[:]).then_inc(S.st, 16)
-    sy.wait_ge(S.st, 16)
-    g.wait_ge(S.sent, left)
+    elif rank == 3:
+        sy.dma_start(X, T.x[:]).then_inc(S.ld, 16)
+        sy.dma_start(T.wdn[:], T.wd[:]).then_inc(S.ldd, 16)
+        g.wait_ge(S.ld, 16)
+        send(2, T.rx3[:], X, S.ax3)
+        send(0, T.rx3[:], X, S.ax3)
+        te.wait_ge(S.ld, 16)
+        te.wait_ge(S.ldd, 16)
+        mm(T.pe, T.wdn[:, 0:W], X, True, False)
+        arrived(S.ade, 2)
+        arrived(S.auv, 0)
+        arrived(S.as2, 2)
+        mm(T.pc, T.ruv[:, W:2 * W], T.rs2[:], True, False)
+        mm(T.pd, T.rde[:, 0:W], T.rs2[:], True, False)
+        arrived(S.as0, 0)
+        mm(T.pc, T.ruv[:, 0:W], T.rs0[:], False, True).then_inc(S.mc, 1)
+        relu(T.t0, T.pc, S.mc, S.vc)
+        te.wait_ge(S.vc, 1)
+        mm(T.pd, T.rde[:, W:2 * W], T.t0[:], False, True).then_inc(S.md, 1)
+        relu(T.t2, T.pd, S.md, S.vd)
+        te.wait_ge(S.vd, 1)
+        mm(T.pe, T.wdn[:, W:2 * W], T.t2[:], False, True).then_inc(S.me, 1)
+        relu(T.yo, T.pe, S.me, S.ve)
+        store(T.yo, S.ve, 1)
+
+    else:
+        sy.dma_start(X, T.x[:]).then_inc(S.ld, 16)
+        sy.dma_start(T.wdn[:], T.wd[:]).then_inc(S.ldd, 16)
+        g.wait_ge(S.ld, 16)
+        send(0, T.rx1[:], X, S.ax1)
+        te.wait_ge(S.ld, 16)
+        te.wait_ge(S.ldd, 16)
+        mm(T.pa, T.wdn[:, 0:W], X, True, False)
+        arrived(S.at0, 0)
+        mm(T.pa, T.wdn[:, W:2 * W], T.rt0[:], False, True).then_inc(S.ma, 1)
+        relu(T.yo, T.pa, S.ma, S.va)
+        store(T.yo, S.va, 1)

from concourse.mybir import AluOpType

TK = 64
W = 128
HALF = TK + 2 * W
PK = TK + 4 * W

SCRATCH = {
    "pk":   ("sbuf", [128, PK], "bfloat16"),
    "wdn":  ("sbuf", [128, 2 * W], "bfloat16"),
    "rp2":  ("sbuf", [128, HALF], "bfloat16"),
    "ruv":  ("sbuf", [128, 2 * W], "bfloat16"),
    "rde":  ("sbuf", [128, 2 * W], "bfloat16"),
    "rx1":  ("sbuf", [128, TK], "bfloat16"),
    "rx3":  ("sbuf", [128, TK], "bfloat16"),
    "rs0":  ("sbuf", [128, TK], "bfloat16"),
    "rs2":  ("sbuf", [128, TK], "bfloat16"),
    "rt0":  ("sbuf", [128, TK], "bfloat16"),
    "s0":   ("sbuf", [128, TK], "bfloat16"),
    "s2":   ("sbuf", [128, TK], "bfloat16"),
    "t0":   ("sbuf", [128, TK], "bfloat16"),
    "t2":   ("sbuf", [128, TK], "bfloat16"),
    "yo":   ("sbuf", [128, TK], "bfloat16"),
    "zero": ("sbuf", [128, TK], "float32"),
    "pa":   ("psum", [128, 512], "float32"),
    "pb":   ("psum", [128, 512], "float32"),
    "pc":   ("psum", [128, 512], "float32"),
    "pd":   ("psum", [128, 512], "float32"),
    "pe":   ("psum", [128, 512], "float32"),
}
SEMAPHORES = ["ld", "lduv", "ldd", "zs", "sent", "st",
              "ax1", "ax3", "ap2", "auv", "ade", "as0", "as2", "at0",
              "ma", "mb", "mc", "md", "me", "va", "vb", "vc", "vd", "ve"]


def rank_program(g, core, T, topo):
    rank = T.rank_of(core)
    if rank is None:
        return
    S = T.sem
    te, ve, sy, sc = g.tensor, g.vector, g.sync, g.scalar
    X = T.pk[:, 0:TK]
    left = [0]

    def tile(buf, k):
        return buf[:, TK + k * W: TK + (k + 1) * W]

    def send(r, out, src, sem):
        dst = T.cores[r]
        rid, pid = topo.addr(dst, core)
        m = topo.mask(core, dst)
        g.remote_dma(out_ap=out, in_ap=src, remote_sem=sem, local_sem=S.sent, pid=pid, routing_id=rid,
                     dma_engine_mask=m)
        left[0] += bin(m).count("1")

    def arrived(sem, r):
        te.wait_ge(sem, bin(topo.mask(T.cores[r], core)).count("1"))

    def mm(acc, w, s, first, last):
        return te.matmul(acc[:, 0:TK], w, s, first, last)

    def relu(out, acc, after, done):
        ve.wait_ge(after, 1)
        ve.tensor_tensor(out[:], acc[:, 0:TK], T.zero[:], AluOpType.max).then_inc(done, 1)

    def store(out, ready, n):
        sy.wait_ge(ready, n)
        sy.dma_start(T.y[:], out[:]).then_inc(S.st, 16)
        sy.wait_ge(S.st, 16)
        g.wait_ge(S.sent, left[0])

    ve.memset(T.zero[:], 0.0).then_inc(S.zs, 1)
    ve.wait_ge(S.zs, 1)

    if rank == 0:
        sc.dma_start(T.pk[:, HALF:PK], T.wu[:, 2 * W:4 * W]).then_inc(S.lduv, 16)
        sy.dma_start(X, T.x[:]).then_inc(S.ld, 16)
        sy.dma_start(T.pk[:, TK:HALF], T.wu[:, 0:2 * W]).then_inc(S.ld, 16)
        g.wait_ge(S.lduv, 16)
        send(3, T.ruv[:], T.pk[:, HALF:PK], S.auv)
        send(2, T.ruv[:], T.pk[:, HALF:PK], S.auv)
        te.wait_ge(S.ld, 32)
        mm(T.pa, tile(T.pk, 0), X, True, False)
        arrived(S.ax1, 1)
        mm(T.pa, tile(T.pk, 1), T.rx1[:], False, True).then_inc(S.ma, 1)
        relu(T.s0, T.pa, S.ma, S.va)
        g.wait_ge(S.va, 1)
        send(3, T.rs0[:], T.s0[:], S.as0)
        send(2, T.rs0[:], T.s0[:], S.as0)
        te.wait_ge(S.va, 1)
        te.wait_ge(S.lduv, 16)
        mm(T.pc, tile(T.pk, 2), T.s0[:], True, False)
        arrived(S.ax3, 3)
        arrived(S.ap2, 2)
        mm(T.pb, tile(T.rp2, 0), T.rp2[:, 0:TK], True, False)
        mm(T.pb, tile(T.rp2, 1), T.rx3[:], False, True).then_inc(S.mb, 1)
        relu(T.s2, T.pb, S.mb, S.vb)
        te.wait_ge(S.vb, 1)
        mm(T.pc, tile(T.pk, 3), T.s2[:], False, True).then_inc(S.mc, 1)
        relu(T.t0, T.pc, S.mc, S.vc)
        g.wait_ge(S.vc, 1)
        send(1, T.rt0[:], T.t0[:], S.at0)
        store(T.t0, S.sent, left[0])

    elif rank == 2:
        sy.dma_start(X, T.x[:]).then_inc(S.ld, 16)
        sc.dma_start(T.pk[:, TK:HALF], T.wu[:, 0:2 * W]).then_inc(S.ld, 16)
        sy.dma_start(T.wdn[:], T.wd[:]).then_inc(S.ldd, 16)
        g.wait_ge(S.ld, 32)
        send(0, T.rp2[:], T.pk[:, 0:HALF], S.ap2)
        g.wait_ge(S.ldd, 16)
        send(3, T.rde[:], T.wdn[:], S.ade)
        te.wait_ge(S.ld, 32)
        mm(T.pb, tile(T.pk, 0), X, True, False)
        arrived(S.ax3, 3)
        mm(T.pb, tile(T.pk, 1), T.rx3[:], False, True).then_inc(S.mb, 1)
        relu(T.s2, T.pb, S.mb, S.vb)
        g.wait_ge(S.vb, 1)
        send(3, T.rs2[:], T.s2[:], S.as2)
        te.wait_ge(S.vb, 1)
        te.wait_ge(S.ldd, 16)
        mm(T.pd, T.wdn[:, 0:W], T.s2[:], True, False)
        arrived(S.auv, 0)
        mm(T.pc, T.ruv[:, W:2 * W], T.s2[:], True, False)
        arrived(S.as0, 0)
        mm(T.pc, T.ruv[:, 0:W], T.rs0[:], False, True).then_inc(S.mc, 1)
        relu(T.t0, T.pc, S.mc, S.vc)
        te.wait_ge(S.vc, 1)
        mm(T.pd, T.wdn[:, W:2 * W], T.t0[:], False, True).then_inc(S.md, 1)
        relu(T.t2, T.pd, S.md, S.vd)
        store(T.t2, S.vd, 1)

    elif rank == 3:
        sy.dma_start(X, T.x[:]).then_inc(S.ld, 16)
        sy.dma_start(T.wdn[:], T.wd[:]).then_inc(S.ldd, 16)
        g.wait_ge(S.ld, 16)
        send(2, T.rx3[:], X, S.ax3)
        send(0, T.rx3[:], X, S.ax3)
        te.wait_ge(S.ld, 16)
        te.wait_ge(S.ldd, 16)
        mm(T.pe, T.wdn[:, 0:W], X, True, False)
        arrived(S.ade, 2)
        arrived(S.auv, 0)
        arrived(S.as2, 2)
        mm(T.pc, T.ruv[:, W:2 * W], T.rs2[:], True, False)
        mm(T.pd, T.rde[:, 0:W], T.rs2[:], True, False)
        arrived(S.as0, 0)
        mm(T.pc, T.ruv[:, 0:W], T.rs0[:], False, True).then_inc(S.mc, 1)
        relu(T.t0, T.pc, S.mc, S.vc)
        te.wait_ge(S.vc, 1)
        mm(T.pd, T.rde[:, W:2 * W], T.t0[:], False, True).then_inc(S.md, 1)
        relu(T.t2, T.pd, S.md, S.vd)
        te.wait_ge(S.vd, 1)
        mm(T.pe, T.wdn[:, W:2 * W], T.t2[:], False, True).then_inc(S.me, 1)
        relu(T.yo, T.pe, S.me, S.ve)
        store(T.yo, S.ve, 1)

    else:
        sy.dma_start(X, T.x[:]).then_inc(S.ld, 16)
        sy.dma_start(T.wdn[:], T.wd[:]).then_inc(S.ldd, 16)
        g.wait_ge(S.ld, 16)
        send(0, T.rx1[:], X, S.ax1)
        te.wait_ge(S.ld, 16)
        te.wait_ge(S.ldd, 16)
        mm(T.pa, T.wdn[:, 0:W], X, True, False)
        arrived(S.at0, 0)
        mm(T.pa, T.wdn[:, W:2 * W], T.rt0[:], False, True).then_inc(S.ma, 1)
        relu(T.yo, T.pa, S.ma, S.va)
        store(T.yo, S.va, 1)
